import numpy as np
import ml_dtypes

BF16 = ml_dtypes.bfloat16


def bf(x):
    return np.asarray(x, np.float32).astype(BF16)


def f32(x):
    return np.asarray(x, np.float32)


def f64(x):
    return np.asarray(x).astype(np.float64)


def striped(idx):
    return np.concatenate([l.reshape(-1, 16).T for l in idx])


def rows(idx, k):
    return np.tile(np.repeat(idx, 16, axis=0), (k // (16 * 8), 1))


def look(tab, idx):
    return np.take_along_axis(f64(tab), rows(idx, len(tab)), axis=1)


K, S, V, N = 256, 2048, 1024, 1024


def setup_inputs():
    return {"tab": f32(np.random.standard_normal((2, K, S))), "th": f32(0.5 * np.random.standard_normal((K, V))), "offs": striped(np.stack([np.random.permutation(S)[:N] for _ in range(8)]))}


def reference(tab, th, offs):
    idx = np.stack([g.T.reshape(-1) for g in np.split(offs, 8)])
    x = (look(tab[0], idx) >= f64(th)) * look(tab[1], idx)
    return x

@@ -1,0 +1,31 @@
+import concourse.mybir as mybir
+
+F32, U16 = mybir.dt.float32, mybir.dt.uint16
+P = 128
+GROUP = 16
+PIECE = 512
+
+
+def tile_lookup_sel_out_kernel(tc, tab, th, offs, out):
+    nc = tc.nc
+    rows, places = tab.shape[1], tab.shape[2]
+    entries = th.shape[1]
+    with tc.tile_pool(name="held", bufs=1) as held:
+        offsets = held.tile([P, entries // GROUP], U16, name="offsets")
+        nc.sync.dma_start(offsets[:], offs)
+        for b in range(rows // P):
+            block = slice(b * P, (b + 1) * P)
+            keys = held.tile([P, places], F32, name=f"keys{b}")
+            thresholds = held.tile([P, entries], F32, name=f"thresholds{b}")
+            values = held.tile([P, places], F32, name=f"values{b}")
+            nc.sync.dma_start(keys[:], tab[0, block, :])
+            nc.sync.dma_start(thresholds[:], th[block, :])
+            nc.sync.dma_start(values[:], tab[1, block, :])
+            for q in range(entries // PIECE):
+                piece = slice(q * PIECE, (q + 1) * PIECE)
+                listed = offsets[:, q * PIECE // GROUP : (q + 1) * PIECE // GROUP]
+                passed = held.tile([P, PIECE], F32, name=f"passed{b}_{q}")
+                kept = held.tile([P, PIECE], F32, name=f"kept{b}_{q}")
+                nc.vector.tensor_tensor(passed[:], keys[:].indirect(listed), thresholds[:, piece], mybir.AluOpType.is_ge)
+                nc.vector.tensor_tensor(kept[:], values[:].indirect(listed), passed[:], mybir.AluOpType.mult)
+                nc.sync.dma_start(out[block, piece], kept[:])

@@ -10,22 +10,30 @@ def tile_lookup_sel_out_kernel(tc, tab, th, offs, out):
     nc = tc.nc
     rows, places = tab.shape[1], tab.shape[2]
     entries = th.shape[1]
+    blocks = [slice(b * P, (b + 1) * P) for b in range(rows // P)]
+    pieces = [slice(q * PIECE, (q + 1) * PIECE) for q in range(entries // PIECE)]
     with tc.tile_pool(name="held", bufs=1) as held:
         offsets = held.tile([P, entries // GROUP], U16, name="offsets")
         nc.sync.dma_start(offsets[:], offs)
-        for b in range(rows // P):
-            block = slice(b * P, (b + 1) * P)
-            keys = held.tile([P, places], F32, name=f"keys{b}")
-            thresholds = held.tile([P, entries], F32, name=f"thresholds{b}")
-            values = held.tile([P, places], F32, name=f"values{b}")
-            nc.sync.dma_start(keys[:], tab[0, block, :])
-            nc.sync.dma_start(thresholds[:], th[block, :])
-            nc.sync.dma_start(values[:], tab[1, block, :])
-            for q in range(entries // PIECE):
-                piece = slice(q * PIECE, (q + 1) * PIECE)
-                listed = offsets[:, q * PIECE // GROUP : (q + 1) * PIECE // GROUP]
-                passed = held.tile([P, PIECE], F32, name=f"passed{b}_{q}")
+
+        keys, thresholds, values = [], [], []
+        for b, block in enumerate(blocks):
+            keys.append(held.tile([P, places], F32, name=f"keys{b}"))
+            values.append(held.tile([P, places], F32, name=f"values{b}"))
+            thresholds.append([held.tile([P, PIECE], F32, name=f"thresholds{b}_{q}") for q in range(len(pieces))])
+            nc.sync.dma_start(keys[b][:], tab[0, block, :])
+            for q, piece in enumerate(pieces):
+                nc.sync.dma_start(thresholds[b][q][:], th[block, piece])
+            nc.sync.dma_start(values[b][:], tab[1, block, :])
+
+        for b, block in enumerate(blocks):
+            passed = []
+            for q, piece in enumerate(pieces):
+                listed = offsets[:, piece.start // GROUP : piece.stop // GROUP]
+                passed.append(held.tile([P, PIECE], F32, name=f"passed{b}_{q}"))
+                nc.vector.tensor_tensor(passed[q][:], keys[b][:].indirect(listed), thresholds[b][q][:], mybir.AluOpType.is_ge)
+            for q, piece in enumerate(pieces):
+                listed = offsets[:, piece.start // GROUP : piece.stop // GROUP]
                 kept = held.tile([P, PIECE], F32, name=f"kept{b}_{q}")
-                nc.vector.tensor_tensor(passed[:], keys[:].indirect(listed), thresholds[:, piece], mybir.AluOpType.is_ge)
-                nc.vector.tensor_tensor(kept[:], values[:].indirect(listed), passed[:], mybir.AluOpType.mult)
+                nc.vector.tensor_tensor(kept[:], values[b][:].indirect(listed), passed[q][:], mybir.AluOpType.mult)
                 nc.sync.dma_start(out[block, piece], kept[:])

@@ -4,6 +4,20 @@ F32, U16 = mybir.dt.float32, mybir.dt.uint16
 P = 128
 GROUP = 16
 PIECE = 512
+LAST = 128
+
+
+def cut(widths):
+    starts = [sum(widths[:i]) for i in range(len(widths))]
+    return [slice(s, s + w) for s, w in zip(starts, widths)]
+
+
+def halving(total, smallest):
+    widths = []
+    while total > smallest:
+        total //= 2
+        widths.append(total)
+    return widths + [smallest]
 
 
 def tile_lookup_sel_out_kernel(tc, tab, th, offs, out):
@@ -11,29 +25,30 @@ def tile_lookup_sel_out_kernel(tc, tab, th, offs, out):
     rows, places = tab.shape[1], tab.shape[2]
     entries = th.shape[1]
     blocks = [slice(b * P, (b + 1) * P) for b in range(rows // P)]
-    pieces = [slice(q * PIECE, (q + 1) * PIECE) for q in range(entries // PIECE)]
+    even_pieces = cut([PIECE] * (entries // PIECE))
     with tc.tile_pool(name="held", bufs=1) as held:
         offsets = held.tile([P, entries // GROUP], U16, name="offsets")
-        nc.sync.dma_start(offsets[:], offs)
+
+        def listed(piece):
+            return offsets[:, piece.start // GROUP : piece.stop // GROUP]
 
         keys, thresholds, values = [], [], []
         for b, block in enumerate(blocks):
             keys.append(held.tile([P, places], F32, name=f"keys{b}"))
             values.append(held.tile([P, places], F32, name=f"values{b}"))
-            thresholds.append([held.tile([P, PIECE], F32, name=f"thresholds{b}_{q}") for q in range(len(pieces))])
+            thresholds.append(held.tile([P, entries], F32, name=f"thresholds{b}"))
             nc.sync.dma_start(keys[b][:], tab[0, block, :])
-            for q, piece in enumerate(pieces):
-                nc.sync.dma_start(thresholds[b][q][:], th[block, piece])
+            if b == 0:
+                nc.sync.dma_start(offsets[:], offs)
+            for piece in even_pieces:
+                nc.sync.dma_start(thresholds[b][:, piece], th[block, piece])
             nc.sync.dma_start(values[b][:], tab[1, block, :])
 
         for b, block in enumerate(blocks):
-            passed = []
-            for q, piece in enumerate(pieces):
-                listed = offsets[:, piece.start // GROUP : piece.stop // GROUP]
-                passed.append(held.tile([P, PIECE], F32, name=f"passed{b}_{q}"))
-                nc.vector.tensor_tensor(passed[q][:], keys[b][:].indirect(listed), thresholds[b][q][:], mybir.AluOpType.is_ge)
-            for q, piece in enumerate(pieces):
-                listed = offsets[:, piece.start // GROUP : piece.stop // GROUP]
-                kept = held.tile([P, PIECE], F32, name=f"kept{b}_{q}")
-                nc.vector.tensor_tensor(kept[:], values[b][:].indirect(listed), passed[q][:], mybir.AluOpType.mult)
-                nc.sync.dma_start(out[block, piece], kept[:])
+            passed = held.tile([P, entries], F32, name=f"passed{b}")
+            kept = held.tile([P, entries], F32, name=f"kept{b}")
+            for piece in even_pieces:
+                nc.vector.tensor_tensor(passed[:, piece], keys[b][:].indirect(listed(piece)), thresholds[b][:, piece], mybir.AluOpType.is_ge)
+            for piece in cut(halving(entries, LAST)) if b == len(blocks) - 1 else even_pieces:
+                nc.vector.tensor_tensor(kept[:, piece], values[b][:].indirect(listed(piece)), passed[:, piece], mybir.AluOpType.mult)
+                nc.sync.dma_start(out[block, piece], kept[:, piece])

import concourse.mybir as mybir

F32, U16 = mybir.dt.float32, mybir.dt.uint16
P = 128
GROUP = 16
PIECE = 512
LAST = 128


def cut(widths):
    starts = [sum(widths[:i]) for i in range(len(widths))]
    return [slice(s, s + w) for s, w in zip(starts, widths)]


def halving(total, smallest):
    widths = []
    while total > smallest:
        total //= 2
        widths.append(total)
    return widths + [smallest]


def tile_lookup_sel_out_kernel(tc, tab, th, offs, out):
    nc = tc.nc
    rows, places = tab.shape[1], tab.shape[2]
    entries = th.shape[1]
    blocks = [slice(b * P, (b + 1) * P) for b in range(rows // P)]
    even_pieces = cut([PIECE] * (entries // PIECE))
    with tc.tile_pool(name="held", bufs=1) as held:
        offsets = held.tile([P, entries // GROUP], U16, name="offsets")

        def listed(piece):
            return offsets[:, piece.start // GROUP : piece.stop // GROUP]

        keys, thresholds, values = [], [], []
        for b, block in enumerate(blocks):
            keys.append(held.tile([P, places], F32, name=f"keys{b}"))
            values.append(held.tile([P, places], F32, name=f"values{b}"))
            thresholds.append(held.tile([P, entries], F32, name=f"thresholds{b}"))
            nc.sync.dma_start(keys[b][:], tab[0, block, :])
            if b == 0:
                nc.sync.dma_start(offsets[:], offs)
            for piece in even_pieces:
                nc.sync.dma_start(thresholds[b][:, piece], th[block, piece])
            nc.sync.dma_start(values[b][:], tab[1, block, :])

        for b, block in enumerate(blocks):
            passed = held.tile([P, entries], F32, name=f"passed{b}")
            kept = held.tile([P, entries], F32, name=f"kept{b}")
            for piece in even_pieces:
                nc.vector.tensor_tensor(passed[:, piece], keys[b][:].indirect(listed(piece)), thresholds[b][:, piece], mybir.AluOpType.is_ge)
            for piece in cut(halving(entries, LAST)) if b == len(blocks) - 1 else even_pieces:
                nc.vector.tensor_tensor(kept[:, piece], values[b][:].indirect(listed(piece)), passed[:, piece], mybir.AluOpType.mult)
                nc.sync.dma_start(out[block, piece], kept[:, piece])
